import numpy as np, ml_dtypes
CORES = [21,29,37,45,53,61,69,77,85]
N = 9
C = 256
def setup_inputs(rng):
    return {"x": rng.standard_normal((N, 128, C), dtype=np.float32).astype(ml_dtypes.bfloat16)}
def setup_inputs_big(rng):
    d = setup_inputs(rng)
    for k in ("x",): d[k] = (d[k].astype(np.float32) * 1048576.0).astype(d[k].dtype)
    return d
def setup_inputs_small(rng):
    d = setup_inputs(rng)
    for k in ("x",): d[k] = (d[k].astype(np.float32) * (1 / 1048576.0)).astype(d[k].dtype)
    return d
def setup_inputs_apart(rng):
    d = setup_inputs(rng)
    f = (10.0 ** rng.permutation(np.linspace(-1.5, 1.5, N))).astype(np.float32).reshape(N, 1, 1)
    for k in ("x",): d[k] = (d[k].astype(np.float32) * f).astype(d[k].dtype)
    return d
def reference(x):
    X = x.astype(np.float64)
    y = np.stack([sum(np.maximum(X[r] - X[s], 0.0) for s in range(N)) for r in range(N)])
    return {"y": y.astype(ml_dtypes.bfloat16)}

@@ -1,0 +1,130 @@
+from concourse.bass import DstId, RemoteDMATransfer
+from concourse.mybir import AluOpType
+
+N = 9
+C = 256
+DIRECT = 2
+
+SCRATCH = {
+    "xd": ("dram", [128, C], "bfloat16"),
+    "relay": ("dram", [128, C], "bfloat16"),
+    "xs": ("sbuf", [128, C], "bfloat16"),
+    "land": ("sbuf", [128, N * C], "bfloat16"),
+    "mins": ("sbuf", [128, N * C], "bfloat16"),
+    "c8": ("sbuf", [128, C], "bfloat16"),
+    "x8": ("sbuf", [128, C], "bfloat16"),
+    "yb": ("sbuf", [128, C], "bfloat16"),
+    "idsrc": ("sbuf", [128, 129], "bfloat16"),
+    "idd": ("dram", [129, 128], "bfloat16"),
+    "ident": ("sbuf", [128, 128], "bfloat16"),
+    "xp": ("psum", [128, 512], "float32"),
+    "acc": ("psum", [128, 512], "float32"),
+}
+SEMAPHORES = (["ldd", "lds", "idw", "idl", "st", "rx", "sent", "vz", "vi", "vc", "vp", "v8", "pe", "vy"]
+              + ["arr%d" % s for s in range(N)] + ["m%d" % k for k in range(N - 1)])
+
+
+def _count(mask):
+    return sum(1 for b in range(mask.bit_length()) if (mask >> b) & 1)
+
+
+def _plan(i, cores, topo):
+    rc = cores[i]
+    chip_cores = [c for c in range(topo.CORES_PER_CHIP * topo.CHIPS) if topo.chip(c) == topo.chip(rc) and c != rc]
+    same = [j for j in range(len(cores)) if j != i and topo.may_write(rc, cores[j])]
+    cross = [j for j in range(len(cores)) if j != i and not topo.may_write(rc, cores[j])]
+    ports = [c for c in chip_cores if all(topo.may_write(c, cores[j]) for j in cross)]
+    plain = [c for c in chip_cores if c not in ports and topo.die(c) != topo.die(rc)]
+    group = sorted(same + [i])
+    a, n = group.index(i), len(group)
+    same = [group[(a + o) % n] for o in range(1, n)]
+    out = [(rc, same[:DIRECT])]
+    for h, j in zip(plain, same[DIRECT:]):
+        out.append((h, [j]))
+    for cls in (0, 1):
+        js = [j for b, j in enumerate(cross) if (a + b) % 2 == cls]
+        ps = [c for c in ports if (topo.die(c) == topo.die(rc)) == (cls == 0)]
+        for k, p in enumerate(ps):
+            if js[k::len(ps)]:
+                out.append((p, js[k::len(ps)]))
+    return out
+
+
+def _write(g, topo, src_core, src, dst_cores, dst, remote_sem, local_sem):
+    mask = topo.mask(src_core, dst_cores[0])
+    for d in dst_cores:
+        mask &= topo.mask(src_core, d)
+    ids = [DstId(rid=topo.addr(d)[0], pnc=topo.addr(d)[1]) for d in dst_cores]
+    g.remote_dma_fused([RemoteDMATransfer(dst_ids=ids, dma_engine_mask=mask, remote_sem=remote_sem,
+                                          srcs=[src], dsts=[dst for _ in dst_cores], alu_op=0)], local_sem=local_sem)
+    return _count(mask)
+
+
+def rank_program(g, core, T, topo):
+    cores = list(T.cores)
+    S = T.sem
+    plans = [_plan(i, cores, topo) for i in range(len(cores))]
+    rank = T.rank_of(core)
+
+    if rank is None:
+        for i, plan in enumerate(plans):
+            for sender, dsts in plan:
+                if sender == core:
+                    g.wait_ge(S.rx, _count(topo.mask(cores[i], core)))
+                    n = _write(g, topo, core, T.relay[:, :], [cores[j] for j in dsts],
+                               T.land[:, i * C:(i + 1) * C], S["arr%d" % i], S.sent)
+                    g.wait_ge(S.sent, n)
+        return
+
+    plan = plans[rank]
+    v, pe = g.vector, g.tensor
+
+    g.sync.dma_start(T.xd[:, :], T.x[:, :]).then_inc(S.ldd, 16)
+    g.scalar.dma_start(T.xs[:, :], T.x[:, :]).then_inc(S.lds, 16)
+
+    g.wait_ge(S.ldd, 16)
+    sent = _write(g, topo, core, T.xd[:, :], [h for h, _ in plan[1:]], T.relay[:, :], S.rx, S.sent)
+    sent += _write(g, topo, core, T.xd[:, :], [cores[j] for j in plan[0][1]],
+                   T.land[:, rank * C:(rank + 1) * C], S["arr%d" % rank], S.sent)
+
+    v.memset(T.idsrc[:, :], 0.0).then_inc(S.vz, 1)
+    v.memset(T.c8[:, :], 8.0).then_inc(S.vc, 1)
+    v.wait_ge(S.vz, 1)
+    v.memset(T.idsrc[:, 0:1], 1.0).then_inc(S.vi, 1)
+    g.scalar.wait_ge(S.vi, 1)
+    g.scalar.dma_start(T.idd[:, :], T.idsrc[:, :]).then_inc(S.idw, 16)
+    g.scalar.wait_ge(S.idw, 16)
+    g.scalar.dma_start(T.ident[:, :], T.idd[0:128, :]).then_inc(S.idl, 16)
+
+    v.wait_ge(S.lds, 16)
+    v.tensor_copy(T.xp[:, 0:C], T.xs[:, :]).then_inc(S.vp, 1)
+    v.wait_ge(S.vc, 1)
+    v.tensor_tensor(T.x8[:, :], T.xs[:, :], T.c8[:, :], op=AluOpType.mult).then_inc(S.v8, 1)
+    v.wait_ge(S.vp, 1)
+
+    arrivals = []
+    for s, p in enumerate(plans):
+        for k, (sender, dsts) in enumerate(p):
+            if rank in dsts:
+                stage = 0 if k == 0 else 1 + dsts.index(rank)
+                arrivals.append((stage, s, _count(topo.mask(sender, core))))
+    arrivals.sort()
+
+    pe.wait_ge(S.idl, 16)
+    last = len(arrivals) - 1
+    for k, (_, s, n) in enumerate(arrivals):
+        v.wait_ge(S["arr%d" % s], n)
+        v.tensor_tensor(T.mins[:, k * C:(k + 1) * C], T.xp[:, 0:C], T.land[:, s * C:(s + 1) * C],
+                        op=AluOpType.min).then_inc(S["m%d" % k], 1)
+        pe.wait_ge(S["m%d" % k], 1)
+        mm = pe.matmul(T.acc[:, 0:C], T.ident[:, :], T.mins[:, k * C:(k + 1) * C], start=(k == 0), stop=(k == last))
+        if k == last:
+            mm.then_inc(S.pe, 1)
+
+    v.wait_ge(S.v8, 1)
+    v.wait_ge(S.pe, 1)
+    v.tensor_tensor(T.yb[:, :], T.x8[:, :], T.acc[:, 0:C], op=AluOpType.subtract).then_inc(S.vy, 1)
+    g.sync.wait_ge(S.vy, 1)
+    g.sync.dma_start(T.y[:, :], T.yb[:, :]).then_inc(S.st, 16)
+    g.sync.wait_ge(S.st, 16)
+    g.wait_ge(S.sent, sent)

@@ -3,7 +3,10 @@ from concourse.mybir import AluOpType
 
 N = 9
 C = 256
-DIRECT = 2
+H = C // 2
+PARTS = 4
+W = 128 // PARTS
+HEAD = 2
 
 SCRATCH = {
     "xd": ("dram", [128, C], "bfloat16"),
@@ -14,13 +17,14 @@ SCRATCH = {
     "c8": ("sbuf", [128, C], "bfloat16"),
     "x8": ("sbuf", [128, C], "bfloat16"),
     "yb": ("sbuf", [128, C], "bfloat16"),
-    "idsrc": ("sbuf", [128, 129], "bfloat16"),
-    "idd": ("dram", [129, 128], "bfloat16"),
+    "idsrc": ("sbuf", [128, W + 1], "bfloat16"),
+    "idd": ("dram", [128 + PARTS, W], "bfloat16"),
     "ident": ("sbuf", [128, 128], "bfloat16"),
     "xp": ("psum", [128, 512], "float32"),
-    "acc": ("psum", [128, 512], "float32"),
+    "acc0": ("psum", [128, 512], "float32"),
+    "acc1": ("psum", [128, 512], "float32"),
 }
-SEMAPHORES = (["ldd", "lds", "idw", "idl", "st", "rx", "sent", "vz", "vi", "vc", "vp", "v8", "pe", "vy"]
+SEMAPHORES = (["ldd", "lds", "idw", "idl", "st", "rx", "sent", "vz", "vi", "vc", "vp", "v8", "pe0", "pe1", "vy", "ml1"]
               + ["arr%d" % s for s in range(N)] + ["m%d" % k for k in range(N - 1)])
 
 
@@ -28,34 +32,65 @@ def _count(mask):
     return sum(1 for b in range(mask.bit_length()) if (mask >> b) & 1)
 
 
-def _plan(i, cores, topo):
-    rc = cores[i]
-    chip_cores = [c for c in range(topo.CORES_PER_CHIP * topo.CHIPS) if topo.chip(c) == topo.chip(rc) and c != rc]
-    same = [j for j in range(len(cores)) if j != i and topo.may_write(rc, cores[j])]
-    cross = [j for j in range(len(cores)) if j != i and not topo.may_write(rc, cores[j])]
-    ports = [c for c in chip_cores if all(topo.may_write(c, cores[j]) for j in cross)]
-    plain = [c for c in chip_cores if c not in ports and topo.die(c) != topo.die(rc)]
-    group = sorted(same + [i])
-    a, n = group.index(i), len(group)
-    same = [group[(a + o) % n] for o in range(1, n)]
-    out = [(rc, same[:DIRECT])]
-    for h, j in zip(plain, same[DIRECT:]):
-        out.append((h, [j]))
-    for cls in (0, 1):
-        js = [j for b, j in enumerate(cross) if (a + b) % 2 == cls]
-        ps = [c for c in ports if (topo.die(c) == topo.die(rc)) == (cls == 0)]
-        for k, p in enumerate(ps):
-            if js[k::len(ps)]:
-                out.append((p, js[k::len(ps)]))
-    return out
+def _split(mask, n):
+    bits = [b for b in range(mask.bit_length()) if (mask >> b) & 1]
+    size = len(bits) // n
+    return [sum(1 << b for b in bits[k * size:(k + 1) * size]) for k in range(n)]
 
 
-def _write(g, topo, src_core, src, dst_cores, dst, remote_sem, local_sem):
-    mask = topo.mask(src_core, dst_cores[0])
-    for d in dst_cores:
-        mask &= topo.mask(src_core, d)
-    ids = [DstId(rid=topo.addr(d)[0], pnc=topo.addr(d)[1]) for d in dst_cores]
-    g.remote_dma_fused([RemoteDMATransfer(dst_ids=ids, dma_engine_mask=mask, remote_sem=remote_sem,
+def _plans(cores, topo):
+    n = len(cores)
+    pairs = [(s, d) for s in range(n) for d in range(n) if s != d]
+    into, mate_port, die_of = {}, {}, {}
+    for s, d in pairs:
+        if topo.may_write(cores[s], cores[d]):
+            key = (d, topo.die(cores[s]))
+            into[key] = into.get(key, 0) + 1
+
+    def are_mates(p):
+        return topo.mates(topo.chip(cores[p[0]]), topo.chip(cores[p[1]]))
+
+    cross = [p for p in pairs if not topo.may_write(cores[p[0]], cores[p[1]])]
+    cross.sort(key=lambda p: (are_mates(p), (p[1] - p[0]) % n, p[0]))
+    for s, d in cross:
+        own = topo.die(cores[s])
+        best = None
+        for e in sorted({topo.die(c) for c in range(topo.CORES_PER_CHIP)}):
+            load = 0 if are_mates((s, d)) else into.get((d, e), 0) + 1 - (HEAD if e == own else 0)
+            key = (max(load, mate_port.get((s, e), 0) + 1), load, mate_port.get((s, e), 0), e != own)
+            if best is None or key < best[0]:
+                best = (key, e)
+        e = best[1]
+        die_of[(s, d)] = e
+        mate_port[(s, e)] = mate_port.get((s, e), 0) + 1
+        if not are_mates((s, d)):
+            into[(d, e)] = into.get((d, e), 0) + 1
+
+    plans = []
+    for i, rc in enumerate(cores):
+        chip_cores = [c for c in range(topo.CORES_PER_CHIP * topo.CHIPS) if topo.chip(c) == topo.chip(rc) and c != rc]
+        same = [j for j in range(n) if j != i and topo.may_write(rc, cores[j])]
+        far = [j for j in range(n) if j != i and not topo.may_write(rc, cores[j])]
+        ports = [c for c in chip_cores if all(topo.may_write(c, cores[j]) for j in far)]
+        group = sorted(same + [i])
+        a = group.index(i)
+        out = [(rc, [group[(a + o) % len(group)] for o in range(1, len(group))])]
+        for e in sorted({topo.die(c) for c in ports}):
+            js = [j for j in far if die_of[(i, j)] == e]
+            ps = [c for c in ports if topo.die(c) == e]
+            for k, p in enumerate(ps):
+                if js[k::len(ps)]:
+                    out.append((p, js[k::len(ps)]))
+        plans.append(out)
+    return plans
+
+
+def _ids(topo, dst_cores):
+    return [DstId(rid=topo.addr(d)[0], pnc=topo.addr(d)[1]) for d in dst_cores]
+
+
+def _write(g, topo, mask, src, dst_cores, dst, remote_sem, local_sem):
+    g.remote_dma_fused([RemoteDMATransfer(dst_ids=_ids(topo, dst_cores), dma_engine_mask=mask, remote_sem=remote_sem,
                                           srcs=[src], dsts=[dst for _ in dst_cores], alu_op=0)], local_sem=local_sem)
     return _count(mask)
 
@@ -63,68 +98,91 @@ def _write(g, topo, src_core, src, dst_cores, dst, remote_sem, local_sem):
 def rank_program(g, core, T, topo):
     cores = list(T.cores)
     S = T.sem
-    plans = [_plan(i, cores, topo) for i in range(len(cores))]
+    plans = _plans(cores, topo)
     rank = T.rank_of(core)
+    v, pe = g.vector, g.tensor
 
     if rank is None:
         for i, plan in enumerate(plans):
-            for sender, dsts in plan:
-                if sender == core:
-                    g.wait_ge(S.rx, _count(topo.mask(cores[i], core)))
-                    n = _write(g, topo, core, T.relay[:, :], [cores[j] for j in dsts],
-                               T.land[:, i * C:(i + 1) * C], S["arr%d" % i], S.sent)
-                    g.wait_ge(S.sent, n)
+            for k, (sender, dsts) in enumerate(plan):
+                if sender != core:
+                    continue
+                away = topo.mask(core, cores[dsts[0]])
+                sent = 0
+                q = k - 1
+                if q < PARTS:
+                    v.memset(T.idsrc[:, :], 0.0).then_inc(S.vz, 1)
+                    v.wait_ge(S.vz, 1)
+                    v.memset(T.idsrc[q * W:(q + 1) * W, 0:1], 1.0).then_inc(S.vi, 1)
+                    g.sync.wait_ge(S.vi, 1)
+                    g.sync.dma_start(T.idd[:, :], T.idsrc[:, :]).then_inc(S.idw, 16)
+                    g.wait_ge(S.idw, 16)
+                    sent += _write(g, topo, away & topo.mask(core, cores[i]), T.idd[q:q + 128, :], [cores[i]],
+                                   T.ident[:, q * W:(q + 1) * W], S.idl, S.sent)
+                g.wait_ge(S.rx, _count(topo.mask(cores[i], core)))
+                g.remote_dma_fused(
+                    [RemoteDMATransfer(dst_ids=_ids(topo, [cores[j]]), dma_engine_mask=m, remote_sem=S["arr%d" % i],
+                                       srcs=[T.relay[:, :]], dsts=[T.land[:, i * C:(i + 1) * C]], alu_op=0)
+                     for j, m in zip(dsts, _split(away, len(dsts)))], local_sem=S.sent)
+                sent += sum(_count(m) for m in _split(away, len(dsts)))
+                g.wait_ge(S.sent, sent)
         return
 
     plan = plans[rank]
-    v, pe = g.vector, g.tensor
+    helpers = [h for h, _ in plan[1:]]
+    mine = [cores[j] for j in plan[0][1]]
 
     g.sync.dma_start(T.xd[:, :], T.x[:, :]).then_inc(S.ldd, 16)
-    g.scalar.dma_start(T.xs[:, :], T.x[:, :]).then_inc(S.lds, 16)
+    g.sync.dma_start(T.xs[:, :], T.x[:, :]).then_inc(S.lds, 16)
 
     g.wait_ge(S.ldd, 16)
-    sent = _write(g, topo, core, T.xd[:, :], [h for h, _ in plan[1:]], T.relay[:, :], S.rx, S.sent)
-    sent += _write(g, topo, core, T.xd[:, :], [cores[j] for j in plan[0][1]],
+    sent = _write(g, topo, topo.mask(core, helpers[0]), T.xd[:, :], helpers, T.relay[:, :], S.rx, S.sent)
+    sent += _write(g, topo, topo.mask(core, mine[0]), T.xd[:, :], mine,
                    T.land[:, rank * C:(rank + 1) * C], S["arr%d" % rank], S.sent)
 
-    v.memset(T.idsrc[:, :], 0.0).then_inc(S.vz, 1)
     v.memset(T.c8[:, :], 8.0).then_inc(S.vc, 1)
-    v.wait_ge(S.vz, 1)
-    v.memset(T.idsrc[:, 0:1], 1.0).then_inc(S.vi, 1)
-    g.scalar.wait_ge(S.vi, 1)
-    g.scalar.dma_start(T.idd[:, :], T.idsrc[:, :]).then_inc(S.idw, 16)
-    g.scalar.wait_ge(S.idw, 16)
-    g.scalar.dma_start(T.ident[:, :], T.idd[0:128, :]).then_inc(S.idl, 16)
-
     v.wait_ge(S.lds, 16)
     v.tensor_copy(T.xp[:, 0:C], T.xs[:, :]).then_inc(S.vp, 1)
     v.wait_ge(S.vc, 1)
     v.tensor_tensor(T.x8[:, :], T.xs[:, :], T.c8[:, :], op=AluOpType.mult).then_inc(S.v8, 1)
     v.wait_ge(S.vp, 1)
+    v.wait_ge(S.v8, 1)
 
     arrivals = []
     for s, p in enumerate(plans):
         for k, (sender, dsts) in enumerate(p):
             if rank in dsts:
-                stage = 0 if k == 0 else 1 + dsts.index(rank)
-                arrivals.append((stage, s, _count(topo.mask(sender, core))))
+                if k == 0:
+                    arrivals.append((0, dsts.index(rank), s, _count(topo.mask(sender, core))))
+                else:
+                    arrivals.append((1, len(dsts), s, _count(_split(topo.mask(sender, core), len(dsts))[0])))
     arrivals.sort()
 
-    pe.wait_ge(S.idl, 16)
+    accs = [T.acc0, T.acc1]
+    pe.wait_ge(S.idl, sum(_count(topo.mask(h, core) & topo.mask(h, cores[d[0]])) for h, d in plan[1:1 + PARTS]))
     last = len(arrivals) - 1
-    for k, (_, s, n) in enumerate(arrivals):
+    for k, (_, _, s, n) in enumerate(arrivals):
         v.wait_ge(S["arr%d" % s], n)
-        v.tensor_tensor(T.mins[:, k * C:(k + 1) * C], T.xp[:, 0:C], T.land[:, s * C:(s + 1) * C],
-                        op=AluOpType.min).then_inc(S["m%d" % k], 1)
-        pe.wait_ge(S["m%d" % k], 1)
-        mm = pe.matmul(T.acc[:, 0:C], T.ident[:, :], T.mins[:, k * C:(k + 1) * C], start=(k == 0), stop=(k == last))
-        if k == last:
-            mm.then_inc(S.pe, 1)
+        if k < last:
+            v.tensor_tensor(T.mins[:, k * C:(k + 1) * C], T.xp[:, 0:C], T.land[:, s * C:(s + 1) * C],
+                            op=AluOpType.min).then_inc(S["m%d" % k], 1)
+            pe.wait_ge(S["m%d" % k], 1)
+            for h in range(2):
+                pe.matmul(accs[h][:, 0:H], T.ident[:, :], T.mins[:, k * C + h * H:k * C + (h + 1) * H],
+                          start=(k == 0), stop=False)
+        else:
+            for h, (ms, ps) in enumerate([(S["m%d" % k], S.pe0), (S.ml1, S.pe1)]):
+                v.tensor_tensor(T.mins[:, k * C + h * H:k * C + (h + 1) * H], T.xp[:, h * H:(h + 1) * H],
+                                T.land[:, s * C + h * H:s * C + (h + 1) * H], op=AluOpType.min).then_inc(ms, 1)
+                pe.wait_ge(ms, 1)
+                pe.matmul(accs[h][:, 0:H], T.ident[:, :], T.mins[:, k * C + h * H:k * C + (h + 1) * H],
+                          start=False, stop=True).then_inc(ps, 1)
 
-    v.wait_ge(S.v8, 1)
-    v.wait_ge(S.pe, 1)
-    v.tensor_tensor(T.yb[:, :], T.x8[:, :], T.acc[:, 0:C], op=AluOpType.subtract).then_inc(S.vy, 1)
-    g.sync.wait_ge(S.vy, 1)
+    for h, ps in enumerate([S.pe0, S.pe1]):
+        v.wait_ge(ps, 1)
+        v.tensor_tensor(T.yb[:, h * H:(h + 1) * H], T.x8[:, h * H:(h + 1) * H], accs[h][:, 0:H],
+                        op=AluOpType.subtract).then_inc(S.vy, 1)
+    g.sync.wait_ge(S.vy, 2)
     g.sync.dma_start(T.y[:, :], T.yb[:, :]).then_inc(S.st, 16)
     g.sync.wait_ge(S.st, 16)
     g.wait_ge(S.sent, sent)

@@ -34,18 +34,21 @@ def _count(mask):
 
 def _split(mask, n):
     bits = [b for b in range(mask.bit_length()) if (mask >> b) & 1]
-    size = len(bits) // n
+    size = 1
+    while size * 2 * n <= len(bits):
+        size *= 2
     return [sum(1 << b for b in bits[k * size:(k + 1) * size]) for k in range(n)]
 
 
 def _plans(cores, topo):
     n = len(cores)
     pairs = [(s, d) for s in range(n) for d in range(n) if s != d]
-    into, mate_port, die_of = {}, {}, {}
+    into, outof, mate_port, die_of = {}, {}, {}, {}
     for s, d in pairs:
         if topo.may_write(cores[s], cores[d]):
-            key = (d, topo.die(cores[s]))
-            into[key] = into.get(key, 0) + 1
+            e = topo.die(cores[s])
+            into[(d, e)] = into.get((d, e), 0) + 1
+            outof[(topo.chip(cores[s]), e)] = outof.get((topo.chip(cores[s]), e), 0) + 1
 
     def are_mates(p):
         return topo.mates(topo.chip(cores[p[0]]), topo.chip(cores[p[1]]))
@@ -54,10 +57,13 @@ def _plans(cores, topo):
     cross.sort(key=lambda p: (are_mates(p), (p[1] - p[0]) % n, p[0]))
     for s, d in cross:
         own = topo.die(cores[s])
+        via = [c for c in range(topo.CHIPS) if topo.mates(topo.chip(cores[s]), c)][0]
         best = None
         for e in sorted({topo.die(c) for c in range(topo.CORES_PER_CHIP)}):
-            load = 0 if are_mates((s, d)) else into.get((d, e), 0) + 1 - (HEAD if e == own else 0)
-            key = (max(load, mate_port.get((s, e), 0) + 1), load, mate_port.get((s, e), 0), e != own)
+            head = HEAD if e == own else 0
+            load = 0 if are_mates((s, d)) else into.get((d, e), 0) + 1 - head
+            leave = 0 if are_mates((s, d)) else outof.get((via, e), 0) + 1 - head
+            key = (max(load, leave, mate_port.get((s, e), 0) + 1), load, mate_port.get((s, e), 0), e != own)
             if best is None or key < best[0]:
                 best = (key, e)
         e = best[1]
@@ -65,6 +71,7 @@ def _plans(cores, topo):
         mate_port[(s, e)] = mate_port.get((s, e), 0) + 1
         if not are_mates((s, d)):
             into[(d, e)] = into.get((d, e), 0) + 1
+            outof[(via, e)] = outof.get((via, e), 0) + 1
 
     plans = []
     for i, rc in enumerate(cores):
@@ -81,6 +88,8 @@ def _plans(cores, topo):
             for k, p in enumerate(ps):
                 if js[k::len(ps)]:
                     out.append((p, js[k::len(ps)]))
+        out[1:] = sorted(out[1:], key=lambda hd: (-mate_port[(i, topo.die(hd[0]))], topo.die(hd[0]) == topo.die(rc),
+                                                  -len(hd[1])))
         plans.append(out)
     return plans
 
@@ -89,10 +98,22 @@ def _ids(topo, dst_cores):
     return [DstId(rid=topo.addr(d)[0], pnc=topo.addr(d)[1]) for d in dst_cores]
 
 
+def _on_mask(topo, cores, plan, helper):
+    return topo.mask(plan[0][0], helper) & ~topo.mask(plan[0][0], cores[plan[0][1][0]])
+
+
 def _write(g, topo, mask, src, dst_cores, dst, remote_sem, local_sem):
     g.remote_dma_fused([RemoteDMATransfer(dst_ids=_ids(topo, dst_cores), dma_engine_mask=mask, remote_sem=remote_sem,
                                           srcs=[src], dsts=[dst for _ in dst_cores], alu_op=0)], local_sem=local_sem)
     return _count(mask)
+
+
+def _fan(g, topo, mask, src, dst_cores, dst, remote_sem, local_sem):
+    shares = _split(mask, len(dst_cores))
+    g.remote_dma_fused([RemoteDMATransfer(dst_ids=_ids(topo, [d]), dma_engine_mask=m, remote_sem=remote_sem,
+                                          srcs=[src], dsts=[dst], alu_op=0) for d, m in zip(dst_cores, shares)],
+                       local_sem=local_sem)
+    return sum(_count(m) for m in shares)
 
 
 def rank_program(g, core, T, topo):
@@ -119,12 +140,9 @@ def rank_program(g, core, T, topo):
                     g.wait_ge(S.idw, 16)
                     sent += _write(g, topo, away & topo.mask(core, cores[i]), T.idd[q:q + 128, :], [cores[i]],
                                    T.ident[:, q * W:(q + 1) * W], S.idl, S.sent)
-                g.wait_ge(S.rx, _count(topo.mask(cores[i], core)))
-                g.remote_dma_fused(
-                    [RemoteDMATransfer(dst_ids=_ids(topo, [cores[j]]), dma_engine_mask=m, remote_sem=S["arr%d" % i],
-                                       srcs=[T.relay[:, :]], dsts=[T.land[:, i * C:(i + 1) * C]], alu_op=0)
-                     for j, m in zip(dsts, _split(away, len(dsts)))], local_sem=S.sent)
-                sent += sum(_count(m) for m in _split(away, len(dsts)))
+                g.wait_ge(S.rx, _count(_on_mask(topo, cores, plan, core)))
+                sent += _fan(g, topo, away, T.relay[:, :], [cores[j] for j in dsts],
+                             T.land[:, i * C:(i + 1) * C], S["arr%d" % i], S.sent)
                 g.wait_ge(S.sent, sent)
         return
 
@@ -136,9 +154,9 @@ def rank_program(g, core, T, topo):
     g.sync.dma_start(T.xs[:, :], T.x[:, :]).then_inc(S.lds, 16)
 
     g.wait_ge(S.ldd, 16)
-    sent = _write(g, topo, topo.mask(core, helpers[0]), T.xd[:, :], helpers, T.relay[:, :], S.rx, S.sent)
-    sent += _write(g, topo, topo.mask(core, mine[0]), T.xd[:, :], mine,
-                   T.land[:, rank * C:(rank + 1) * C], S["arr%d" % rank], S.sent)
+    sent = _write(g, topo, _on_mask(topo, cores, plan, helpers[0]), T.xd[:, :], helpers, T.relay[:, :], S.rx, S.sent)
+    sent += _fan(g, topo, topo.mask(core, mine[0]), T.xd[:, :], mine,
+                 T.land[:, rank * C:(rank + 1) * C], S["arr%d" % rank], S.sent)
 
     v.memset(T.c8[:, :], 8.0).then_inc(S.vc, 1)
     v.wait_ge(S.lds, 16)
@@ -152,10 +170,8 @@ def rank_program(g, core, T, topo):
     for s, p in enumerate(plans):
         for k, (sender, dsts) in enumerate(p):
             if rank in dsts:
-                if k == 0:
-                    arrivals.append((0, dsts.index(rank), s, _count(topo.mask(sender, core))))
-                else:
-                    arrivals.append((1, len(dsts), s, _count(_split(topo.mask(sender, core), len(dsts))[0])))
+                engines = _count(_split(topo.mask(sender, core), len(dsts))[0])
+                arrivals.append((min(k, 1), k + 2 * (len(dsts) - 1) if k else dsts.index(rank), s, engines))
     arrivals.sort()
 
     accs = [T.acc0, T.acc1]

from concourse.bass import DstId, RemoteDMATransfer
from concourse.mybir import AluOpType

N = 9
C = 256
H = C // 2
PARTS = 4
W = 128 // PARTS
HEAD = 2

SCRATCH = {
    "xd": ("dram", [128, C], "bfloat16"),
    "relay": ("dram", [128, C], "bfloat16"),
    "xs": ("sbuf", [128, C], "bfloat16"),
    "land": ("sbuf", [128, N * C], "bfloat16"),
    "mins": ("sbuf", [128, N * C], "bfloat16"),
    "c8": ("sbuf", [128, C], "bfloat16"),
    "x8": ("sbuf", [128, C], "bfloat16"),
    "yb": ("sbuf", [128, C], "bfloat16"),
    "idsrc": ("sbuf", [128, W + 1], "bfloat16"),
    "idd": ("dram", [128 + PARTS, W], "bfloat16"),
    "ident": ("sbuf", [128, 128], "bfloat16"),
    "xp": ("psum", [128, 512], "float32"),
    "acc0": ("psum", [128, 512], "float32"),
    "acc1": ("psum", [128, 512], "float32"),
}
SEMAPHORES = (["ldd", "lds", "idw", "idl", "st", "rx", "sent", "vz", "vi", "vc", "vp", "v8", "pe0", "pe1", "vy", "ml1"]
              + ["arr%d" % s for s in range(N)] + ["m%d" % k for k in range(N - 1)])


def _count(mask):
    return sum(1 for b in range(mask.bit_length()) if (mask >> b) & 1)


def _split(mask, n):
    bits = [b for b in range(mask.bit_length()) if (mask >> b) & 1]
    size = 1
    while size * 2 * n <= len(bits):
        size *= 2
    return [sum(1 << b for b in bits[k * size:(k + 1) * size]) for k in range(n)]


def _plans(cores, topo):
    n = len(cores)
    pairs = [(s, d) for s in range(n) for d in range(n) if s != d]
    into, outof, mate_port, die_of = {}, {}, {}, {}
    for s, d in pairs:
        if topo.may_write(cores[s], cores[d]):
            e = topo.die(cores[s])
            into[(d, e)] = into.get((d, e), 0) + 1
            outof[(topo.chip(cores[s]), e)] = outof.get((topo.chip(cores[s]), e), 0) + 1

    def are_mates(p):
        return topo.mates(topo.chip(cores[p[0]]), topo.chip(cores[p[1]]))

    cross = [p for p in pairs if not topo.may_write(cores[p[0]], cores[p[1]])]
    cross.sort(key=lambda p: (are_mates(p), (p[1] - p[0]) % n, p[0]))
    for s, d in cross:
        own = topo.die(cores[s])
        via = [c for c in range(topo.CHIPS) if topo.mates(topo.chip(cores[s]), c)][0]
        best = None
        for e in sorted({topo.die(c) for c in range(topo.CORES_PER_CHIP)}):
            head = HEAD if e == own else 0
            load = 0 if are_mates((s, d)) else into.get((d, e), 0) + 1 - head
            leave = 0 if are_mates((s, d)) else outof.get((via, e), 0) + 1 - head
            key = (max(load, leave, mate_port.get((s, e), 0) + 1), load, mate_port.get((s, e), 0), e != own)
            if best is None or key < best[0]:
                best = (key, e)
        e = best[1]
        die_of[(s, d)] = e
        mate_port[(s, e)] = mate_port.get((s, e), 0) + 1
        if not are_mates((s, d)):
            into[(d, e)] = into.get((d, e), 0) + 1
            outof[(via, e)] = outof.get((via, e), 0) + 1

    plans = []
    for i, rc in enumerate(cores):
        chip_cores = [c for c in range(topo.CORES_PER_CHIP * topo.CHIPS) if topo.chip(c) == topo.chip(rc) and c != rc]
        same = [j for j in range(n) if j != i and topo.may_write(rc, cores[j])]
        far = [j for j in range(n) if j != i and not topo.may_write(rc, cores[j])]
        ports = [c for c in chip_cores if all(topo.may_write(c, cores[j]) for j in far)]
        group = sorted(same + [i])
        a = group.index(i)
        out = [(rc, [group[(a + o) % len(group)] for o in range(1, len(group))])]
        for e in sorted({topo.die(c) for c in ports}):
            js = [j for j in far if die_of[(i, j)] == e]
            ps = [c for c in ports if topo.die(c) == e]
            for k, p in enumerate(ps):
                if js[k::len(ps)]:
                    out.append((p, js[k::len(ps)]))
        out[1:] = sorted(out[1:], key=lambda hd: (-mate_port[(i, topo.die(hd[0]))], topo.die(hd[0]) == topo.die(rc),
                                                  -len(hd[1])))
        plans.append(out)
    return plans


def _ids(topo, dst_cores):
    return [DstId(rid=topo.addr(d)[0], pnc=topo.addr(d)[1]) for d in dst_cores]


def _on_mask(topo, cores, plan, helper):
    return topo.mask(plan[0][0], helper) & ~topo.mask(plan[0][0], cores[plan[0][1][0]])


def _write(g, topo, mask, src, dst_cores, dst, remote_sem, local_sem):
    g.remote_dma_fused([RemoteDMATransfer(dst_ids=_ids(topo, dst_cores), dma_engine_mask=mask, remote_sem=remote_sem,
                                          srcs=[src], dsts=[dst for _ in dst_cores], alu_op=0)], local_sem=local_sem)
    return _count(mask)


def _fan(g, topo, mask, src, dst_cores, dst, remote_sem, local_sem):
    shares = _split(mask, len(dst_cores))
    g.remote_dma_fused([RemoteDMATransfer(dst_ids=_ids(topo, [d]), dma_engine_mask=m, remote_sem=remote_sem,
                                          srcs=[src], dsts=[dst], alu_op=0) for d, m in zip(dst_cores, shares)],
                       local_sem=local_sem)
    return sum(_count(m) for m in shares)


def rank_program(g, core, T, topo):
    cores = list(T.cores)
    S = T.sem
    plans = _plans(cores, topo)
    rank = T.rank_of(core)
    v, pe = g.vector, g.tensor

    if rank is None:
        for i, plan in enumerate(plans):
            for k, (sender, dsts) in enumerate(plan):
                if sender != core:
                    continue
                away = topo.mask(core, cores[dsts[0]])
                sent = 0
                q = k - 1
                if q < PARTS:
                    v.memset(T.idsrc[:, :], 0.0).then_inc(S.vz, 1)
                    v.wait_ge(S.vz, 1)
                    v.memset(T.idsrc[q * W:(q + 1) * W, 0:1], 1.0).then_inc(S.vi, 1)
                    g.sync.wait_ge(S.vi, 1)
                    g.sync.dma_start(T.idd[:, :], T.idsrc[:, :]).then_inc(S.idw, 16)
                    g.wait_ge(S.idw, 16)
                    sent += _write(g, topo, away & topo.mask(core, cores[i]), T.idd[q:q + 128, :], [cores[i]],
                                   T.ident[:, q * W:(q + 1) * W], S.idl, S.sent)
                g.wait_ge(S.rx, _count(_on_mask(topo, cores, plan, core)))
                sent += _fan(g, topo, away, T.relay[:, :], [cores[j] for j in dsts],
                             T.land[:, i * C:(i + 1) * C], S["arr%d" % i], S.sent)
                g.wait_ge(S.sent, sent)
        return

    plan = plans[rank]
    helpers = [h for h, _ in plan[1:]]
    mine = [cores[j] for j in plan[0][1]]

    g.sync.dma_start(T.xd[:, :], T.x[:, :]).then_inc(S.ldd, 16)
    g.sync.dma_start(T.xs[:, :], T.x[:, :]).then_inc(S.lds, 16)

    g.wait_ge(S.ldd, 16)
    sent = _write(g, topo, _on_mask(topo, cores, plan, helpers[0]), T.xd[:, :], helpers, T.relay[:, :], S.rx, S.sent)
    sent += _fan(g, topo, topo.mask(core, mine[0]), T.xd[:, :], mine,
                 T.land[:, rank * C:(rank + 1) * C], S["arr%d" % rank], S.sent)

    v.memset(T.c8[:, :], 8.0).then_inc(S.vc, 1)
    v.wait_ge(S.lds, 16)
    v.tensor_copy(T.xp[:, 0:C], T.xs[:, :]).then_inc(S.vp, 1)
    v.wait_ge(S.vc, 1)
    v.tensor_tensor(T.x8[:, :], T.xs[:, :], T.c8[:, :], op=AluOpType.mult).then_inc(S.v8, 1)
    v.wait_ge(S.vp, 1)
    v.wait_ge(S.v8, 1)

    arrivals = []
    for s, p in enumerate(plans):
        for k, (sender, dsts) in enumerate(p):
            if rank in dsts:
                engines = _count(_split(topo.mask(sender, core), len(dsts))[0])
                arrivals.append((min(k, 1), k + 2 * (len(dsts) - 1) if k else dsts.index(rank), s, engines))
    arrivals.sort()

    accs = [T.acc0, T.acc1]
    pe.wait_ge(S.idl, sum(_count(topo.mask(h, core) & topo.mask(h, cores[d[0]])) for h, d in plan[1:1 + PARTS]))
    last = len(arrivals) - 1
    for k, (_, _, s, n) in enumerate(arrivals):
        v.wait_ge(S["arr%d" % s], n)
        if k < last:
            v.tensor_tensor(T.mins[:, k * C:(k + 1) * C], T.xp[:, 0:C], T.land[:, s * C:(s + 1) * C],
                            op=AluOpType.min).then_inc(S["m%d" % k], 1)
            pe.wait_ge(S["m%d" % k], 1)
            for h in range(2):
                pe.matmul(accs[h][:, 0:H], T.ident[:, :], T.mins[:, k * C + h * H:k * C + (h + 1) * H],
                          start=(k == 0), stop=False)
        else:
            for h, (ms, ps) in enumerate([(S["m%d" % k], S.pe0), (S.ml1, S.pe1)]):
                v.tensor_tensor(T.mins[:, k * C + h * H:k * C + (h + 1) * H], T.xp[:, h * H:(h + 1) * H],
                                T.land[:, s * C + h * H:s * C + (h + 1) * H], op=AluOpType.min).then_inc(ms, 1)
                pe.wait_ge(ms, 1)
                pe.matmul(accs[h][:, 0:H], T.ident[:, :], T.mins[:, k * C + h * H:k * C + (h + 1) * H],
                          start=False, stop=True).then_inc(ps, 1)

    for h, ps in enumerate([S.pe0, S.pe1]):
        v.wait_ge(ps, 1)
        v.tensor_tensor(T.yb[:, h * H:(h + 1) * H], T.x8[:, h * H:(h + 1) * H], accs[h][:, 0:H],
                        op=AluOpType.subtract).then_inc(S.vy, 1)
    g.sync.wait_ge(S.vy, 2)
    g.sync.dma_start(T.y[:, :], T.yb[:, :]).then_inc(S.st, 16)
    g.sync.wait_ge(S.st, 16)
    g.wait_ge(S.sent, sent)
